import numpy as np
import ml_dtypes


def mxq(x, axis, fmt="e4m3"):
    dtype, down = {"e4m3": (ml_dtypes.float8_e4m3fn, 7), "e5m2": (ml_dtypes.float8_e5m2, 14)}[fmt]
    v = np.moveaxis(np.asarray(x, np.float32).astype(ml_dtypes.bfloat16).astype(np.float64), axis, -1)
    blocks = v.reshape(v.shape[:-1] + (-1, 32))
    amax = np.abs(blocks).max(-1, keepdims=True)
    byte = np.maximum(np.where(amax > 0, np.frexp(amax)[1] - 1 + 127, 0) - down, 1)
    scale = np.exp2(byte - 127.0)
    codes = (blocks / scale).astype(np.float32).astype(dtype).astype(np.float64)
    return np.moveaxis((codes * scale).reshape(v.shape), -1, axis)


WIDE = False


def mx_kscale(k):
    if not WIDE:
        return np.ones(k)
    levels = np.array([10, -10, 5, -5, 0])
    if k % 512:
        return np.exp2(np.random.permutation(np.resize(levels, k // 32))).repeat(32)
    a = np.empty((k // 512, 16))
    for p in range(k // 512):
        a[p, :8] = np.random.permutation(np.resize(levels, 8))
        for g in range(8):
            far = levels[np.abs(levels - a[p, g]) >= 10]
            a[p, g + 8] = far[np.random.randint(len(far))]
    return np.exp2(a.ravel()).repeat(32)


BF16 = ml_dtypes.bfloat16


def bf(x):
    return np.asarray(x, np.float32).astype(BF16)


def f64(x):
    return np.asarray(x).astype(np.float64)


V, D, H = 1024, 1024, 1536


def sigmoid(z):
    return 0.5 * (1.0 + np.tanh(0.5 * z))


def draw0():
    s = mx_kscale(D)
    t = mx_kscale(V)
    return {"x": bf(np.random.standard_normal((V, D)) * s),
            "a": bf(np.random.standard_normal((V, D)) / np.sqrt(D) / s),
            "beta": bf(0.5 * np.random.standard_normal(V)),
            "c": bf(np.random.standard_normal((V, V)) * t),
            "w": bf(np.random.standard_normal((D, H)) / np.sqrt(D) / s[:, None]),
            "b": bf(0.3 * np.random.standard_normal(H)),
            "d": bf((1.0 + 0.1 * np.random.standard_normal(V)) / t),
            "r": bf(1.0 + 0.1 * np.random.standard_normal(H)),
            "h": bf(0.3 * np.random.standard_normal((V, H)))}


def core(x, a, beta, c, w, b, d, r, h):
    xq = mxq(f64(x), 1, "e4m3")
    e = (mxq(f64(a), 1, "e4m3") @ xq.T) + f64(beta)[:, None]
    gate = sigmoid(e)
    degree = np.sum(gate, axis=1, keepdims=True)
    g = gate * f64(c)
    z = (xq @ mxq(f64(w), 0, "e4m3")) + f64(b)
    m = z * sigmoid(z) * f64(d)[:, None]
    agg = mxq(g, 1, "e4m3") @ mxq(m, 0, "e4m3")
    return f64(h) + f64(r) * agg / np.sqrt(degree)


def e4m3fn_bytes(y):
    return np.clip(np.asarray(y, np.float64), -448.0, 448.0).astype(np.float32).astype(ml_dtypes.float8_e4m3fn).view(np.uint8)


def e4m3fn_values(b):
    return np.asarray(b, np.uint8).view(ml_dtypes.float8_e4m3fn).astype(np.float64)


def setup_inputs():
    d = draw0()
    x0 = np.asarray(d['w']).astype(np.float64)
    s = (np.max(np.abs(x0), axis=(1,), keepdims=True) / 448.0).astype(np.float32)
    out = {}
    for k, v in d.items():
        if k == 'w':
            out['w_bytes'] = e4m3fn_bytes(x0 / s.astype(np.float64))
            out['w_scale'] = s
        else:
            out[k] = v
    return out


def reference(x, a, beta, c, w_bytes, w_scale, b, d, r, h):
    return core(x, a, beta, c, e4m3fn_values(w_bytes) * w_scale.astype(np.float64), b, d, r, h)

from contextlib import ExitStack

import concourse.mybir as mybir
from concourse.masks import make_identity

V, D, H = 1024, 1024, 1536
P = 128
FLOPS = 2 * V * D * V + 2 * V * D * H + 2 * V * V * H

F32 = mybir.dt.float32
BF16 = mybir.dt.bfloat16
U32 = mybir.dt.uint32
U8 = mybir.dt.uint8
FP8 = mybir.dt.float8_e4m3fn
FP8X4 = mybir.dt.float8_e4m3fn_x4
ACT = mybir.ActivationFunctionType
ALU = mybir.AluOpType


def tile_edge_gated_message_passing_f5_kernel(
    tc, x, a, beta, c, w_bytes, w_scale, b, d, r, h, out
):
    nc = tc.nc
    with ExitStack() as ctx:
        keep = ctx.enter_context(tc.tile_pool(name="keep", bufs=1))
        work = ctx.enter_context(tc.tile_pool(name="work", bufs=2))
        psum = ctx.enter_context(tc.psum_pool(name="psum", bufs=1))
        ctx.enter_context(tc.manual_schedule())

        ident = keep.tile([P, P], F32, name="ident")
        warm = keep.tile([P, 1], F32, name="warm")
        half = keep.tile([P, 1], F32, name="half")
        vt = keep.tile([P, P], BF16, name="vt")
        vf = keep.tile([P, P], F32, name="vf")
        cols = keep.tile([P, 80], F32, name="cols")
        ws = keep.tile([P, 2, 4], F32, name="ws")
        dt4 = keep.tile([P, 2, 4], BF16, name="dt4")
        rb = keep.tile([P, H], BF16, name="rb")
        deg = keep.tile([P, 16], F32, name="deg")
        dsum = keep.tile([P, 8], F32, name="dsum")
        rs = keep.tile([P, 8], F32, name="rs")
        wb = keep.tile([P, 2, 4, H], U8, name="wb")
        xr = keep.tile([P, 2, 4, D], BF16, name="xr")
        cr = keep.tile([P, 8, V], BF16, name="cr")
        xq = keep.tile([P, 2, V], U32, name="xq", align_bytes=64)
        xs = keep.tile([P, 2, V], U8, name="xs", align_bytes=64)
        wq = keep.tile([P, 2, H], U32, name="wq", align_bytes=64)
        wqs = keep.tile([P, 2, H], U8, name="wqs", align_bytes=64)
        mq = keep.tile([P, 2, H], U32, name="mq", align_bytes=64)
        mqs = keep.tile([P, 2, H], U8, name="mqs", align_bytes=64)
        aq = keep.tile([P, 8, 256], U32, name="aq", align_bytes=64)
        aqs = keep.tile([P, 8, 256], U8, name="aqs", align_bytes=64)

        nc.vector.memset(vt[:], 0.0)
        nc.vector.memset(warm[:], 0.0)
        nc.gpsimd.memset(half[:], -0.5)
        make_identity(nc, ident[:])

        w_view = w_bytes.rearrange("(g p t) n -> p g t n", g=2, p=P, t=4)
        x_view = x.rearrange("(g m t) k -> g m t k", g=2, m=P, t=4)

        def load_w(g, lo, hi):
            nc.sync.dma_start(out=wb[:, g, :, lo:hi], in_=w_view[:, g, :, lo:hi])

        def load_x(g, t):
            nc.sync.dma_start(out=xr[:, g, t, :], in_=x_view[g][:, t, :])

        load_w(0, 0, 512)
        load_w(1, 0, 512)
        nc.scalar.dma_start(out=ws[:], in_=w_scale.rearrange("(g p t) o -> p g (t o)", g=2, p=P, t=4))
        nc.scalar.activation(out=warm[:], in_=warm[:], func=ACT.Silu)
        nc.gpsimd.dma_start(out=vt[0:12, :], in_=b.rearrange("(n p) -> n p", p=P))
        nc.gpsimd.dma_start(out=vt[32:40, :], in_=beta.rearrange("(n p) -> n p", p=P))
        nc.gpsimd.dma_start(out=vt[64:76, :], in_=r.rearrange("(n p) -> n p", p=P))
        nc.gpsimd.dma_start(out=dt4[:], in_=d.rearrange("(g p t) -> p g t", g=2, p=P, t=4))
        for t in range(4):
            load_x(0, t)
        load_w(0, 512, H)
        for t in range(4):
            load_x(1, t)
        load_w(1, 512, H)
        ar = {}
        hr = {}

        def load_a(i):
            at = work.tile([P, D], BF16, name="at", bufs=4)
            nc.sync.dma_start(out=at[:], in_=a[i * P : (i + 1) * P, :])
            ar[i] = at

        def load_h(i):
            ht = work.tile([P, H], BF16, name="ht", bufs=5)
            nc.sync.dma_start(out=ht[:], in_=h[i * P : (i + 1) * P, :])
            hr[i] = ht

        for i in range(4):
            load_a(i)
        for i in range(2):
            nc.sync.dma_start(out=cr[:, i, :], in_=c[i * P : (i + 1) * P, :])
        nc.sync.dma_start(out=rb[:], in_=r.partition_broadcast(P))
        for i in range(8):
            if i >= 2:
                nc.sync.dma_start(out=cr[:, i, :], in_=c[i * P : (i + 1) * P, :])
            if i < 5:
                load_h(i)

        def copy(engine, dst, src):
            if engine == 0:
                nc.scalar.copy(dst, src)
            else:
                nc.vector.tensor_copy(out=dst, in_=src)

        def bank_tr():
            return psum.tile([P, 4, P], F32, name="tr", bufs=3)

        def bank_mm():
            return psum.tile([P, 512], F32, name="mm", bufs=5)

        def words_transposed(words, step2):
            bank = bank_tr()
            for j in range(4):
                if step2:
                    src = words[:, 256 * (j // 2) + j % 2 : 256 * (j // 2 + 1) : 2]
                else:
                    src = words[:, P * j : P * (j + 1)]
                nc.tensor.transpose(bank[:, j, :], src, ident[:])
            return bank

        xg = {}

        def x_turn(g, t, engine):
            if t == 0:
                xg[g] = work.tile([P, 2, 512, 2], F32, name="xg", bufs=2, align_bytes=64)
            bank = words_transposed(xr[:, g, t, :].bitcast(F32), True)
            copy(engine, xg[g][:, :, t * P : (t + 1) * P, :], bank[:].rearrange("p (q u) m -> p q m u", u=2))

        def x_quant(g, q):
            nc.vector.quantize_mx(
                out=xq[:, q, g * 512 : (g + 1) * 512].bitcast(FP8X4),
                scales=xs[:, q, g * 512 : (g + 1) * 512],
                in_=xg[g][:].rearrange("p q m u -> p (q m u)")[:, q * 1024 : (q + 1) * 1024].bitcast(BF16),
            )

        wide = {}

        def w_widen(n3, g, t, engine):
            if t == 0:
                wide[n3, g] = work.tile([P, 4, 512], BF16, name="wide", bufs=4, align_bytes=64)
            src = wb[:, g, t, n3 * 512 : (n3 + 1) * 512].bitcast(FP8)
            if engine == 0:
                nc.scalar.activation(out=wide[n3, g][:, t, :], in_=src, func=ACT.Copy, scale=ws[:, g, t : t + 1])
            else:
                nc.vector.tensor_scalar(
                    out=wide[n3, g][:, t, :], in0=src, scalar1=ws[:, g, t : t + 1], scalar2=None, op0=ALU.mult
                )

        wgr = {}

        def w_inter(n3, g, engine):
            wgr[n3, g] = work.tile([P, 512, 4], BF16, name="wgr", bufs=2, align_bytes=64)
            dst = wgr[n3, g][:].rearrange("p (n i) t -> p n t i", i=4)
            src = wide[n3, g][:].rearrange("p t (n i) -> p n t i", i=4)
            if engine == 1:
                nc.vector.tensor_copy(out=dst, in_=src)
            else:
                nc.gpsimd.tensor_scalar(out=dst, in0=src, scalar1=1.0, scalar2=0.0, op0=ALU.mult, op1=ALU.add)

        def w_quant(n3, g):
            nc.vector.quantize_mx(
                out=wq[:, g, n3 * 512 : (n3 + 1) * 512].bitcast(FP8X4),
                scales=wqs[:, g, n3 * 512 : (n3 + 1) * 512],
                in_=wgr[n3, g][:].rearrange("p n t -> p (n t)"),
            )

        def mx(bank, lhs, rhs):
            for q in range(2):
                lt, ls = lhs(q)
                rt, rsc = rhs(q)
                nc.tensor.matmul_mx(
                    out=bank,
                    lhsT=lt.bitcast(FP8X4),
                    lhsT_scale=ls,
                    rhs=rt.bitcast(FP8X4),
                    rhs_scale=rsc,
                    start=(q == 0),
                    stop=(q == 1),
                )

        zb = {}

        def z_mm(blk, g):
            bank = bank_mm()
            nb = slice(blk * P, (blk + 1) * P)
            jb = slice(g * 512, (g + 1) * 512)
            mx(bank[:], lambda q: (wq[:, q, nb], wqs[:, q, nb]), lambda q: (xq[:, q, jb], xs[:, q, jb]))
            zb[blk, g] = bank

        sl = {}

        def silu(blk, g):
            st = work.tile([P, 512], F32, name="st", bufs=6)
            nc.scalar.activation(out=st[:], in_=zb[blk, g][:], func=ACT.Silu, bias=cols[:, blk : blk + 1])
            sl[blk, g] = st

        mg = {}
        mtr = {}

        def m_turn(blk, g):
            mtr[blk, g] = words_transposed(sl[blk, g][:], False)

        def m_mul(blk, g):
            n3 = blk // 4
            if blk % 4 == 0:
                mg[n3, g] = work.tile([P, 512, 4], BF16, name="mgr", bufs=2, align_bytes=64)
            o = (blk % 4) * P
            nc.vector.tensor_tensor(
                out=mg[n3, g][:, o : o + P, :],
                in0=mtr[blk, g][:].rearrange("p t n -> p n t"),
                in1=dt4[:, g, :].unsqueeze(1).to_broadcast([P, P, 4]),
                op=ALU.mult,
            )

        def m_quant(n3, g):
            nc.vector.quantize_mx(
                out=mq[:, g, n3 * 512 : (n3 + 1) * 512].bitcast(FP8X4),
                scales=mqs[:, g, n3 * 512 : (n3 + 1) * 512],
                in_=mg[n3, g][:].rearrange("p n t -> p (n t)"),
            )

        ag = {}

        def a_turn(i):
            bank = words_transposed(ar[i][:].bitcast(F32), True)
            ag[i] = work.tile([P, 2, P, 2], F32, name="agr", bufs=2, align_bytes=64)
            copy(0, ag[i][:], bank[:].rearrange("p (q u) m -> p q m u", u=2))
            if i + 4 < 8:
                load_a(i + 4)

        def a_quant(i):
            nc.vector.quantize_mx(
                out=aq[:, i, :].bitcast(FP8X4),
                scales=aqs[:, i, :],
                in_=ag[i][:].rearrange("p q m u -> p (q m u)").bitcast(BF16),
            )

        gate = {}
        eb = {}

        def e_mm(i, g):
            bank = bank_mm()
            jb = slice(g * 512, (g + 1) * 512)
            mx(
                bank[:],
                lambda q: (aq[:, i, q * P : (q + 1) * P], aqs[:, i, q * P : (q + 1) * P]),
                lambda q: (xq[:, q, jb], xs[:, q, jb]),
            )
            eb[i, g] = bank

        def sig(i, g):
            gt = work.tile([P, 512], F32, name="gt", bufs=4)
            nc.scalar.activation(
                out=gt[:],
                in_=eb[i, g][:],
                func=ACT.Sigmoid,
                bias=cols[:, 32 + i : 33 + i],
                accum_out=deg[:, 2 * i + g : 2 * i + g + 1],
            )
            gate[i, g] = gt

        gw = {}

        def g_mul(i, g):
            if g == 0:
                gw[i] = work.tile([P, V], BF16, name="gw", bufs=3, align_bytes=64)
            nc.vector.tensor_tensor(
                out=gw[i][:, g * 512 : (g + 1) * 512].rearrange("p (u m e) -> p u m e", u=2, e=2),
                in0=gate[i, g][:].rearrange("p (u e m) -> p u m e", u=2, e=2),
                in1=cr[:, i, g * 512 : (g + 1) * 512].rearrange("p (m u e) -> p u m e", u=2, e=2),
                op=ALU.mult,
            )

        def root(i):
            nc.gpsimd.tensor_tensor(
                out=dsum[:, i : i + 1], in0=deg[:, 2 * i : 2 * i + 1], in1=deg[:, 2 * i + 1 : 2 * i + 2], op=ALU.add
            )
            nc.gpsimd.tensor_tensor(out=rs[:, i : i + 1], in0=dsum[:, i : i + 1], in1=half[:], op=ALU.pow)

        gg = {}
        gq = {}

        def g_turn(i):
            bank = words_transposed(gw[i][:].bitcast(F32), False)
            gg[i] = work.tile([P, 2, P, 2], F32, name="ggr", bufs=2, align_bytes=64)
            copy(0, gg[i][:], bank[:].rearrange("p (q u) m -> p q m u", u=2))

        def g_quant(i):
            if i % 2 == 0:
                codes = work.tile([P, 2, 256], U32, name="gqc", bufs=3, align_bytes=64)
                scales = work.tile([P, 2, 256], U8, name="gqs", bufs=3, align_bytes=64)
                gq[i // 2] = (codes, scales)
            codes, scales = gq[i // 2]
            words = gg[i][:].rearrange("p q m u -> p (q m u)")
            ib = slice((i % 2) * P, (i % 2 + 1) * P)
            for q in range(2):
                nc.vector.quantize_mx(
                    out=codes[:, q, ib].bitcast(FP8X4),
                    scales=scales[:, q, ib],
                    in_=words[:, q * 256 : (q + 1) * 256].bitcast(BF16),
                )

        ab = {}

        def agg_mm(i, n3):
            bank = bank_mm()
            codes, scales = gq[i // 2]
            nb = slice(n3 * 512, (n3 + 1) * 512)
            ib = slice((i % 2) * P, (i % 2 + 1) * P)
            mx(bank[:], lambda q: (codes[:, q, ib], scales[:, q, ib]), lambda q: (mq[:, q, nb], mqs[:, q, nb]))
            ab[i, n3] = bank

        et = {}

        def turned_mm(batch, pair):
            bank = bank_mm()
            ev = work.tile([P, 2, 256], F32, name="ev", bufs=4)
            et[batch, pair] = ev
            codes, scales = gq[batch]
            for j in range(2):
                nb = slice((2 * pair + j) * P, (2 * pair + j + 1) * P)
                mx(
                    bank[:, j * 256 : (j + 1) * 256],
                    lambda q: (mq[:, q, nb], mqs[:, q, nb]),
                    lambda q: (codes[:, q, :], scales[:, q, :]),
                )
            for j in range(2):
                blk = 2 * pair + j
                nc.scalar.activation(
                    out=ev[:, j, :],
                    in_=bank[:, j * 256 : (j + 1) * 256],
                    func=ACT.Copy,
                    scale=cols[:, 64 + blk : 65 + blk],
                )

        def turned_back(i):
            bank = bank_tr()
            o = (i % 2) * P
            for j in range(4):
                nc.tensor.transpose(bank[:, j, :], et[i // 2, 4 + j // 2][:, j % 2, o : o + P], ident[:])
            ab[i, 2] = bank

        def finish_turned(i):
            yt[i, 2] = work.tile([P, 512], F32, name="yt", bufs=7)
            nc.vector.scalar_tensor_tensor(
                out=yt[i, 2][:],
                in0=ab[i, 2][:].rearrange("p j n -> p (j n)"),
                scalar=rs[:, i : i + 1],
                in1=hr[i][:, 1024:1536],
                op0=ALU.mult,
                op1=ALU.add,
            )
            store(i, 2)

        yt = {}

        def store(i, n3):
            nc.sync.dma_start(out=out[i * P : (i + 1) * P, n3 * 512 : (n3 + 1) * 512], in_=yt[i, n3][:])

        def scale_out(i, n3):
            yt[i, n3] = work.tile([P, 512], F32, name="yt", bufs=7)
            nb = slice(n3 * 512, (n3 + 1) * 512)
            nc.vector.scalar_tensor_tensor(
                out=yt[i, n3][:], in0=ab[i, n3][:], scalar=rs[:, i : i + 1], in1=rb[:, nb], op0=ALU.mult, op1=ALU.mult
            )

        def h_add(i, n3, engine):
            nb = slice(n3 * 512, (n3 + 1) * 512)
            eng = nc.vector if engine == 1 else nc.gpsimd
            eng.tensor_tensor(out=yt[i, n3][:], in0=yt[i, n3][:], in1=hr[i][:, nb], op=ALU.add)
            store(i, n3)

        for t in range(4):
            w_widen(0, 0, t, 0)
        for t in range(4):
            w_widen(0, 1, t, 1)
        w_inter(0, 1, 1)
        for t in range(4):
            x_turn(0, t, 0)
        w_inter(0, 0, 1)
        w_quant(0, 1)
        w_quant(0, 0)
        units = [(n3, g, t) for n3 in (1, 2) for g in range(2) for t in range(4)]

        def widen_next(count):
            for n in range(count):
                if units:
                    n3, g, t = units[0]
                    units.remove((n3, g, t))
                    w_widen(n3, g, t, 0)

        widen_next(2)
        x_quant(0, 0)
        x_quant(0, 1)
        for t in range(4):
            x_turn(1, t, 0)
        nc.vector.tensor_copy(out=vf[:], in_=vt[:])
        vbank = bank_tr()
        nc.tensor.transpose(vbank[:, 0, :], vf[:], ident[:])
        nc.vector.tensor_copy(out=cols[:], in_=vbank[:, 0, 0:80])

        blocks = [(n3 * 4 + j, g) for n3 in range(3) for g in range(2) for j in range(4)]
        groups = [blocks[4 * k : 4 * k + 4] for k in range(6)]
        halves = ((1, 0), (1, 1), (2, 0), (2, 1))
        for k in range(7):
            if k < 6:
                for blk, g in groups[k]:
                    z_mm(blk, g)
                widen_next(2)
                for blk, g in groups[k]:
                    silu(blk, g)
            if k == 0:
                x_quant(1, 0)
                x_quant(1, 1)
            if k < 4:
                w_inter(halves[k][0], halves[k][1], 1)
            if k > 0:
                for blk, g in groups[k - 1]:
                    m_turn(blk, g)
                    m_mul(blk, g)
            if k < 4:
                w_quant(halves[k][0], halves[k][1])
            if k in (4, 5):
                a_turn(2 * k - 8)
                a_turn(2 * k - 7)
            if k > 0:
                m_quant(groups[k - 1][0][0] // 4, groups[k - 1][0][1])
            if k in (4, 5):
                a_quant(2 * k - 8)
                a_quant(2 * k - 7)
            if k < 6:
                widen_next(2)
            if k == 5:
                e_mm(0, 0)

        def gate_step(i):
            if i > 0:
                e_mm(i, 0)
            e_mm(i, 1)
            sig(i, 0)
            sig(i, 1)
            root(i)
            g_mul(i, 0)
            g_mul(i, 1)

        TURNED = (0, 1, 2)
        gate_step(0)
        gate_step(1)
        for k in range(9):
            back = (k - 3, k - 2) if k % 2 == 1 and (k - 3) // 2 in TURNED else ()
            if k < 8:
                g_turn(k)
            if k < 4:
                a_turn(k + 4)
            for i in back:
                turned_back(i)
            if k < 8:
                g_quant(k)
            if k < 4:
                a_quant(k + 4)
            if k + 2 < 8:
                gate_step(k + 2)
            if k >= 1:
                i = k - 1
                direct = 2 if i // 2 in TURNED else 3
                for n3 in range(direct):
                    agg_mm(i, n3)
                for n3 in range(direct):
                    scale_out(i, n3)
                    if n3 == 0:
                        h_add(i, 0, 2)
            for i in back:
                finish_turned(i)
            if k >= 1:
                for n3 in range(1, direct):
                    h_add(k - 1, n3, 1)
            if k % 2 == 0 and (k - 2) // 2 in TURNED:
                for pair in range(4, 6):
                    turned_mm((k - 2) // 2, pair)
            done = list(back)
            if k >= 1 and (k - 1) // 2 not in TURNED:
                done.extend([k - 1])
            for i in done:
                if i + 5 < 8:
                    load_h(i + 5)
